import numpy as np
import ml_dtypes


def mxq(x, axis, fmt="e4m3"):
    dtype, down = {"e4m3": (ml_dtypes.float8_e4m3fn, 7), "e5m2": (ml_dtypes.float8_e5m2, 14)}[fmt]
    v = np.moveaxis(np.asarray(x, np.float32).astype(ml_dtypes.bfloat16).astype(np.float64), axis, -1)
    blocks = v.reshape(v.shape[:-1] + (-1, 32))
    amax = np.abs(blocks).max(-1, keepdims=True)
    byte = np.maximum(np.where(amax > 0, np.frexp(amax)[1] - 1 + 127, 0) - down, 1)
    scale = np.exp2(byte - 127.0)
    codes = (blocks / scale).astype(np.float32).astype(dtype).astype(np.float64)
    return np.moveaxis((codes * scale).reshape(v.shape), -1, axis)


WIDE = False


def mx_kscale(k):
    if not WIDE:
        return np.ones(k)
    levels = np.array([10, -10, 5, -5, 0])
    if k % 512:
        return np.exp2(np.random.permutation(np.resize(levels, k // 32))).repeat(32)
    a = np.empty((k // 512, 16))
    for p in range(k // 512):
        a[p, :8] = np.random.permutation(np.resize(levels, 8))
        for g in range(8):
            far = levels[np.abs(levels - a[p, g]) >= 10]
            a[p, g + 8] = far[np.random.randint(len(far))]
    return np.exp2(a.ravel()).repeat(32)


def f64(x):
    return np.asarray(x).astype(np.float64)


def striped(idx):
    return np.tile(idx.reshape(-1, 16).T, (8, 1)).astype(np.uint16)


def unstriped(offs):
    return offs[:16].T.reshape(-1).astype(np.int64)


E2M1 = np.array([0.0, 0.5, 1.0, 1.5, 2.0, 3.0, 4.0, 6.0, -0.0, -0.5, -1.0, -1.5, -2.0, -3.0, -4.0, -6.0])


def pack_weight(w, fmt):
    k, n = w.shape
    w = f64(np.asarray(w, np.float32).astype(ml_dtypes.bfloat16)).reshape(k // 32, 32, n)
    amax = np.abs(w).max(1)
    if fmt == "e4m3":
        byte = np.frexp(amax)[1] - 1 + 127 - 7
    else:
        mant, ex = np.frexp(amax / 6.0)
        byte = np.where(mant > 0.5, ex, ex - 1) + 127
    byte = np.clip(np.where(amax > 0, byte, 1), 1, 254)
    scaled = (w * np.exp2(127.0 - byte)[:, None, :]).reshape(k, n).astype(np.float32)
    by_word = np.ascontiguousarray(scaled.reshape(k // 512, 128, 4, n).transpose(0, 1, 3, 2))
    if fmt == "e4m3":
        words = by_word.astype(ml_dtypes.float8_e4m3fn).view(np.uint8)
    else:
        c = by_word.astype(ml_dtypes.float4_e2m1fn).view(np.uint8) & 0xF
        words = (c[..., 0::2] | (c[..., 1::2] << 4)).reshape(k // 512, 128, 2 * n)
    return np.ascontiguousarray(words), np.ascontiguousarray(byte.astype(np.uint8).reshape(k // 512, 16, n))


def unpack_weight(words, scales, fmt):
    g, _, n = scales.shape
    words = np.ascontiguousarray(words).reshape(g, 128, n, -1)
    if fmt == "e4m3":
        vals = words.view(ml_dtypes.float8_e4m3fn).astype(np.float64)
    else:
        nib = np.empty((g, 128, n, 4), np.uint8)
        nib[..., 0::2] = words & 0xF
        nib[..., 1::2] = words >> 4
        vals = E2M1[nib]
    vals = vals * np.repeat(np.exp2(scales.astype(np.float64) - 127.0), 8, axis=1)[..., None]
    return vals.transpose(0, 1, 3, 2).reshape(g * 512, n)


def gelu(v):
    return 0.5 * v * (1.0 + np.tanh(np.sqrt(2.0 / np.pi) * (v + 0.044715 * v**3)))


T, S, K, H, T2, P = 2048, 512, 1024, 1024, 1024, 512


def setup_inputs():
    n = np.random.standard_normal
    s = mx_kscale(K)[:, None]
    u = mx_kscale(H)[:, None]
    tab_words, tab_scales = pack_weight(n((K, T)) * s, "e4m3")
    wgen_words, wgen_scales = pack_weight(0.8 * n((K, H)) / s * u.T / np.sqrt(K), "e2m1")
    wtor = (0.6 * n((K, H)) / s * u.T / np.sqrt(K)).astype(np.float32)
    wph_words, wph_scales = pack_weight(0.55 * n((K, H)) / s / np.sqrt(K), "e4m3")
    return {
        "tab_words": tab_words, "tab_scales": tab_scales,
        "wgen_words": wgen_words, "wgen_scales": wgen_scales,
        "wtor": wtor,
        "wph_words": wph_words, "wph_scales": wph_scales,
        "page0": (n((H, T2)) * u).astype(np.float32),
        "wgs": np.exp(0.3 * n((128, S))).astype(np.float32),
        "base": (0.6 * n(H) * u[:, 0]).astype(np.float32),
        "bal": (n(H) / u[:, 0] ** 2 / np.sqrt(H)).astype(np.float32),
        "cls": (0.7 * n(P)).astype(np.float32),
        "plume": np.random.uniform(0.5, 1.5, P).astype(np.float32),
        "offs": striped(np.random.permutation(T)[:S]),
        "offs2": striped(np.random.permutation(T2)[:S]),
        "offs3": striped(np.random.permutation(T2)[:P]),
        "offs4": striped(np.random.permutation(T2)[:P]),
    }


def reference(tab_words, tab_scales, wgen_words, wgen_scales, wtor, wph_words, wph_scales,
              page0, wgs, base, bal, cls, plume, offs, offs2, offs3, offs4):
    v = unpack_weight(tab_words, tab_scales, "e4m3")[:, unstriped(offs)]
    wgen = unpack_weight(wgen_words, wgen_scales, "e2m1")
    wph = unpack_weight(wph_words, wph_scales, "e4m3")
    f = wgen.T @ v + mxq(f64(wtor), 0, "e4m3").T @ v
    h = f * np.cos(wph.T @ v)
    page = f64(page0).copy()
    page[:, unstriped(offs2)] = np.tile(f64(wgs), (H // 128, 1)) * h
    x1 = page[:, unstriped(offs3)]
    x2 = (page[:, unstriped(offs4)] - f64(base)[:, None]) * f64(bal)[:, None]
    e = mxq(x1, 0, "e4m3").T @ mxq(x2, 0, "e4m3")
    return np.maximum(e, f64(cls)[None, :]) * f64(plume)[:, None]

@@ -1,0 +1,346 @@
+import math
+from contextlib import ExitStack
+
+import concourse.mybir as mybir
+from concourse.masks import make_identity
+
+T, S, K, H, T2, PL = 2048, 512, 1024, 1024, 1024, 512
+FLOPS = 3 * 2 * K * H * S + 2 * H * PL * PL
+
+F32 = mybir.dt.float32
+BF16 = mybir.dt.bfloat16
+I32 = mybir.dt.int32
+U32 = mybir.dt.uint32
+U16 = mybir.dt.uint16
+U8 = mybir.dt.uint8
+FP8X4 = mybir.dt.float8_e4m3fn_x4
+FP4X4 = mybir.dt.float4_e2m1fn_x4
+ALU = mybir.AluOpType
+ACT = mybir.ActivationFunctionType
+
+P = 128
+PACK = 4
+PASS = P * PACK
+RUN = 8
+GROUPS = P // RUN
+QUADS = 4
+TURN_OFFSET = float(2**14)
+
+
+def tile_list_plume_quality_match_kernel(
+    tc, tab_words, tab_scales, wgen_words, wgen_scales, wtor, wph_words, wph_scales,
+    page0, wgs, base, bal, cls, plume, offs, offs2, offs3, offs4, out,
+):
+    nc = tc.nc
+    k_passes = K // PASS
+    r_passes = H // PASS
+
+    with ExitStack() as ctx:
+        keep = ctx.enter_context(tc.tile_pool(name="keep", bufs=1))
+        ring = ctx.enter_context(tc.tile_pool(name="ring", bufs=2))
+        psum = ctx.enter_context(tc.psum_pool(name="psum", bufs=8))
+
+        def bank(name):
+            return psum.tile([P, 512], F32, name=name, tag="bank")
+
+        def wide_f32(name):
+            return ring.tile([P, PACK, 512], F32, name=name, tag="wide_f32", bufs=6)
+
+        lists = {}
+        for name in ("offs", "offs2", "offs3", "offs4"):
+            lists[name] = keep.tile([P, S // 16], U16, name=name)
+        tab_w = [keep.tile([P, T], I32, name=f"tab_w{a}") for a in range(k_passes)]
+        tab_s = keep.tile([P, k_passes, T], U8, name="tab_s")
+        wph_s = keep.tile([P, k_passes, H], U8, name="wph_s")
+        wgen_s = keep.tile([P, k_passes, H], U8, name="wgen_s")
+        wph_raw = [keep.tile([P, k_passes, PASS], I32, name=f"wph_raw{b}", tag="wph_raw") for b in range(r_passes)]
+        wgen_raw = [keep.tile([P, k_passes, PASS // 2], I32, name=f"wgen_raw{b}") for b in range(r_passes)]
+        wtor_raw = {}
+        for b in range(r_passes):
+            for a in range(k_passes):
+                wtor_raw[b, a] = wide_f32(f"wtor_raw{b}{a}")
+        wgs_sb = [keep.tile([P, S], F32, name=f"wgs{t}") for t in range(PACK)]
+        page = {}
+        for b in range(r_passes):
+            for t in range(PACK):
+                page[b, t] = keep.tile([P, T2], F32, name=f"page{b}{t}")
+        rows = keep.tile([P, r_passes * P], F32, name="rows")
+        ident = keep.tile([P, P], F32, name="ident")
+        cls_sb = keep.tile([P, PL], F32, name="cls_sb")
+
+        nc.vector.memset(tab_s[:].rearrange("p a n -> p (a n)").bitcast(I32), 0)
+        nc.vector.memset(wph_s[:].rearrange("p a n -> p (a n)").bitcast(I32), 0)
+        nc.vector.memset(wgen_s[:].rearrange("p a n -> p (a n)").bitcast(I32), 0)
+
+        def load_list(name, src):
+            nc.sync.dma_start(lists[name][:], src)
+
+        def load_scales(queue, dst, src):
+            for q in range(QUADS):
+                queue.dma_start(
+                    out=dst[32 * q : 32 * q + 4, :, :].bitcast(I32),
+                    in_=src[:, 4 * q : 4 * q + 4, :].rearrange("a r n -> r a n").bitcast(I32),
+                )
+
+        def load_table(a):
+            nc.sync.dma_start(out=tab_w[a][:], in_=tab_words[a].rearrange("p n t -> p (n t)").bitcast(I32))
+
+        def load_wph(b):
+            words = wph_words.rearrange("a p n t -> p a (n t)")[:, :, 4 * PASS * b : 4 * PASS * (b + 1)]
+            nc.sync.dma_start(out=wph_raw[b][:], in_=words.bitcast(I32))
+
+        def load_wgen(b):
+            words = wgen_words.rearrange("a p n -> p a n")[:, :, 2 * PASS * b : 2 * PASS * (b + 1)]
+            nc.sync.dma_start(out=wgen_raw[b][:], in_=words.bitcast(I32))
+
+        def load_wtor(b, a):
+            src = wtor[PASS * a : PASS * (a + 1), PASS * b : PASS * (b + 1)]
+            nc.sync.dma_start(out=wtor_raw[b, a][:], in_=src.rearrange("(p j) c -> p j c", j=PACK))
+
+        def load_wgs(queue, t, quads=range(QUADS)):
+            src = wgs.rearrange("(g t i) c -> t g i c", t=PACK, i=RUN)[t]
+            for q in quads:
+                queue.dma_start(out=wgs_sb[t][32 * q : 32 * (q + 1), :], in_=src)
+
+        def load_page(b, t):
+            src = page0[PASS * b : PASS * (b + 1), :].rearrange("(g t i) c -> t g i c", t=PACK, i=RUN)[t]
+            nc.sync.dma_start(out=page[b, t][:], in_=src)
+
+        def load_rows():
+            for row0, vec in ((0, base), (PACK, bal)):
+                nc.sync.dma_start(
+                    out=rows[row0 : row0 + PACK, :].rearrange("t (g i) -> t g i", i=RUN),
+                    in_=vec.rearrange("(g t i) -> t g i", t=PACK, i=RUN),
+                )
+            nc.sync.dma_start(out=rows[2 * PACK : 3 * PACK, 0:P], in_=plume.rearrange("(m p) -> m p", p=P))
+
+        load_wgs(nc.gpsimd, 0, (2, 3))
+        load_wgs(nc.gpsimd, 1)
+        nc.gpsimd.memset(rows[:], 0.0)
+        make_identity(nc, ident[:])
+        load_list("offs", offs)
+        load_list("offs2", offs2)
+        load_list("offs4", offs4)
+        load_list("offs3", offs3)
+        load_wgs(nc.sync, 0, (0, 1))
+        load_table(0)
+        load_table(1)
+        load_scales(nc.scalar, tab_s, tab_scales)
+        load_wph(0)
+        load_wtor(0, 0)
+        load_scales(nc.scalar, wph_s, wph_scales)
+        load_wgen(0)
+        load_wtor(0, 1)
+        load_scales(nc.sync, wgen_s, wgen_scales)
+        load_page(0, 0)
+        load_page(0, 1)
+        load_wph(1)
+        load_wgen(1)
+        load_wtor(1, 0)
+        load_wtor(1, 1)
+        for t in (2, 3):
+            load_page(0, t)
+            load_wgs(nc.sync, t)
+        load_rows()
+        for t in range(PACK):
+            load_page(1, t)
+        nc.sync.dma_start(out=cls_sb[:], in_=cls.partition_broadcast(P))
+
+        v_w = [keep.tile([P, S], U32, name=f"v_w{a}", align_bytes=64) for a in range(k_passes)]
+        v_s = [keep.tile([P, S], U8, name=f"v_s{a}", align_bytes=64) for a in range(k_passes)]
+        for a in range(k_passes):
+            nc.vector.tensor_copy(v_s[a][:], tab_s[:, a, :].indirect(lists["offs"][:]))
+        for a in range(k_passes):
+            nc.vector.tensor_copy(v_w[a][:], tab_w[a][:].bitcast(U32).indirect(lists["offs"][:]))
+
+        def deal(name, raw, words):
+            dealt = keep.tile([P, k_passes, PACK, GROUPS * words], I32, name=name, align_bytes=64)
+            nc.vector.tensor_copy(
+                out=dealt[:].rearrange("p a t (g w) -> p a t g w", w=words),
+                in_=raw.rearrange("p a (g t w) -> p a t g w", t=PACK, w=words),
+            )
+            return dealt
+
+        wph_sb, wgen_sb, wph_sc, wgen_sc, wtor_q, wtor_s, cosine = {}, {}, {}, {}, {}, {}, {}
+
+        def deal_phase(b):
+            wph_sb[b] = deal(f"wph_d{b}", wph_raw[b][:], RUN)
+            wph_sc[b] = deal(f"wph_sd{b}", wph_s[:, :, PASS * b : PASS * (b + 1)].bitcast(I32), 2)
+
+        def deal_gen(b):
+            wgen_sb[b] = deal(f"wgen_d{b}", wgen_raw[b][:], RUN // 2)
+            wgen_sc[b] = deal(f"wgen_sd{b}", wgen_s[:, :, PASS * b : PASS * (b + 1)].bitcast(I32), 2)
+
+        def quantise_wtor(b, pieces, copy, tag=None):
+            name = f"wtor{b}_{pieces[0][0]}{pieces[0][1]}"
+            woven = keep.tile([P, len(pieces) * 512], BF16, name=name + "_bf", tag=tag or name + "_bf", align_bytes=64)
+            codes = keep.tile([P, len(pieces) * P], U32, name=name + "_q", align_bytes=64)
+            scales = keep.tile([P, len(pieces) * P], U8, name=name + "_s", align_bytes=64)
+            for n, (a, t) in enumerate(pieces):
+                copy(
+                    out=woven[:, 512 * n : 512 * (n + 1)].rearrange("p (g h i j) -> p g h j i", h=2, i=4, j=PACK),
+                    in_=wtor_raw[b, a][:].rearrange("p j (g t h i) -> p t g h j i", t=PACK, h=2, i=4)[:, t],
+                )
+                wtor_q[b, a, t] = codes[:, P * n : P * (n + 1)]
+                wtor_s[b, a, t] = scales[:, P * n : P * (n + 1)]
+            nc.vector.quantize_mx(out=codes[:].bitcast(FP8X4), scales=scales[:], in_=woven[:])
+
+        def phase(b, t):
+            z = bank(f"z{b}{t}")
+            for a in range(k_passes):
+                nc.tensor.matmul_mx(
+                    out=z[:],
+                    lhsT=wph_sb[b][:, a, t, :].bitcast(FP8X4),
+                    lhsT_scale=wph_sc[b][:, a, t, :].bitcast(U8),
+                    rhs=v_w[a][:].bitcast(FP8X4),
+                    rhs_scale=v_s[a][:],
+                    start=(a == 0),
+                    stop=(a == k_passes - 1),
+                )
+            turns = ring.tile([P, S], U32, name="turns")
+            nc.scalar.activation(turns[:], z[:], ACT.Copy, bias=TURN_OFFSET, scale=1.0 / (2.0 * math.pi))
+            shift = ring.tile([P, S], F32, name="shift", tag="shift")
+            nc.scalar.activation(shift[:], turns[:], ACT.Copy, bias=2.0 * math.pi * TURN_OFFSET, scale=-2.0 * math.pi)
+            folded = keep.tile([P, S], F32, name=f"folded{b}{t}", tag=f"work{t % 2}", align_bytes=64)
+            nc.vector.tensor_tensor(folded[:], z[:], shift[:], ALU.add)
+            size = ring.tile([P, S], F32, name="size")
+            nc.scalar.activation(size[:], folded[:], ACT.Abs)
+            cosine[b, t] = keep.tile([P, S], F32, name=f"cosine{b}{t}", tag=f"cosine{b}{t}", align_bytes=64)
+            nc.scalar.activation(cosine[b, t][:], size[:], ACT.Sin, bias=math.pi / 2.0, scale=-1.0)
+
+        picked1, picked2 = {}, {}
+
+        def write_and_pick(b, t):
+            f = bank(f"f{b}{t}")
+            for a in range(k_passes):
+                nc.tensor.matmul_mx(
+                    out=f[:],
+                    lhsT=wgen_sb[b][:, a, t, :].bitcast(U8).bitcast(FP4X4),
+                    lhsT_scale=wgen_sc[b][:, a, t, :].bitcast(U8),
+                    rhs=v_w[a][:].bitcast(FP8X4),
+                    rhs_scale=v_s[a][:],
+                    start=(a == 0),
+                    stop=False,
+                )
+            for a in range(k_passes):
+                nc.tensor.matmul_mx(
+                    out=f[:],
+                    lhsT=wtor_q[b, a, t].bitcast(FP8X4),
+                    lhsT_scale=wtor_s[b, a, t],
+                    rhs=v_w[a][:].bitcast(FP8X4),
+                    rhs_scale=v_s[a][:],
+                    start=False,
+                    stop=(a == k_passes - 1),
+                )
+            last = (b, t) == (r_passes - 1, PACK - 1)
+            gained = keep.tile([P, S], F32, name=f"gained{b}{t}", tag="gained13" if last else f"work{t % 2}", align_bytes=64)
+            nc.vector.tensor_tensor(gained[:], f[:], wgs_sb[t][:], ALU.mult)
+            nc.vector.tensor_tensor(page[b, t][:].indirect(lists["offs2"][:]), gained[:], cosine[b, t][:], ALU.mult)
+            if t == 0:
+                picked1[b] = wide_f32(f"picked1_{b}")
+                picked2[b] = wide_f32(f"picked2_{b}")
+            nc.vector.tensor_copy(picked2[b][:, t, :], page[b, t][:].indirect(lists["offs4"][:]))
+            nc.vector.tensor_copy(picked1[b][:, t, :], page[b, t][:].indirect(lists["offs3"][:]))
+
+        cols = keep.tile([P, r_passes, 16], F32, name="cols")
+        neg_bb = keep.tile([P, r_passes, PACK], F32, name="neg_bb")
+        e = []
+
+        def turn_rows():
+            turned = bank("turned")
+            for b in range(r_passes):
+                nc.tensor.transpose(turned[:, P * b : P * (b + 1)], rows[:, P * b : P * (b + 1)], ident[:])
+            nc.scalar.copy(out=cols[:, 0, 0 : 3 * PACK], in_=turned[:, 0 : 3 * PACK])
+            nc.scalar.copy(out=cols[:, 1, 0 : 2 * PACK], in_=turned[:, P : P + 2 * PACK])
+            nc.vector.scalar_tensor_tensor(
+                out=neg_bb[:], in0=cols[:, :, 0:PACK], scalar=-1.0, in1=cols[:, :, PACK : 2 * PACK],
+                op0=ALU.mult, op1=ALU.mult,
+            )
+            for m in range(PL // P):
+                e.append(bank(f"e{m}"))
+
+        def weave(woven, planes, count):
+            nc.scalar.copy(
+                out=woven[:].rearrange("p (c i t) -> p c t i", i=4, t=PACK)[:, :, 0:count, :],
+                in_=planes[:, 0:count, :].rearrange("p t (c i) -> p c t i", i=4),
+            )
+
+        def centre_x2(dst, b, t):
+            nc.scalar.activation(
+                dst, picked2[b][:, t, :], ACT.Identity,
+                bias=neg_bb[:, b, t : t + 1], scale=cols[:, b, PACK + t : PACK + t + 1],
+            )
+
+        def score(b, x2_tag, x1_tag):
+            early = PACK if b + 1 < r_passes else PACK - 1
+            x2_planes = ring.tile([P, PACK, PL], BF16, name="x2_planes")
+            x2_bf = keep.tile([P, PACK * PL], BF16, name=f"x2_bf{b}", tag=x2_tag, align_bytes=64)
+            x1_bf = keep.tile([P, PACK * PL], BF16, name=f"x1_bf{b}", tag=x1_tag, align_bytes=64)
+            x1_q = keep.tile([P, PL], U32, name=f"x1_q{b}", align_bytes=64)
+            x1_s = keep.tile([P, PL], U8, name=f"x1_s{b}", align_bytes=64)
+            x2_q = keep.tile([P, PL], U32, name=f"x2_q{b}", align_bytes=64)
+            x2_s = keep.tile([P, PL], U8, name=f"x2_s{b}", align_bytes=64)
+            for t in range(early):
+                centre_x2(x2_planes[:, t, :], b, t)
+            weave(x2_bf, x2_planes, early)
+            weave(x1_bf, picked1[b], early)
+            for t in range(early, PACK):
+                centre_x2(x2_bf[:].rearrange("p (c t) -> p t c", t=PACK)[:, t, :], b, t)
+            nc.vector.quantize_mx(out=x2_q[:].bitcast(FP8X4), scales=x2_s[:], in_=x2_bf[:])
+            width = PL if early == PACK else P
+            for c0 in range(0, PL, width):
+                for t in range(early, PACK):
+                    nc.scalar.copy(
+                        out=x1_bf[:].rearrange("p (c t) -> p t c", t=PACK)[:, t, c0 : c0 + width],
+                        in_=picked1[b][:, t, c0 : c0 + width],
+                    )
+                nc.vector.quantize_mx(
+                    out=x1_q[:, c0 : c0 + width].bitcast(FP8X4), scales=x1_s[:, c0 : c0 + width],
+                    in_=x1_bf[:, PACK * c0 : PACK * (c0 + width)],
+                )
+            for m in range(PL // P):
+                nc.tensor.matmul_mx(
+                    out=e[m][:],
+                    lhsT=x1_q[:, P * m : P * (m + 1)].bitcast(FP8X4),
+                    lhsT_scale=x1_s[:, P * m : P * (m + 1)],
+                    rhs=x2_q[:].bitcast(FP8X4),
+                    rhs_scale=x2_s[:],
+                    start=(b == 0),
+                    stop=(b == r_passes - 1),
+                )
+
+        deal_phase(0)
+        phase(0, 0)
+        quantise_wtor(0, [(0, 0)], nc.vector.tensor_copy)
+        deal_gen(0)
+        quantise_wtor(0, [(1, 0)], nc.vector.tensor_copy)
+        phase(0, 1)
+        quantise_wtor(0, [(0, 1), (1, 1)], nc.scalar.copy)
+        write_and_pick(0, 0)
+        quantise_wtor(0, [(a, t) for t in (2, 3) for a in range(k_passes)], nc.scalar.copy, "cosine00")
+        phase(0, 2)
+        deal_phase(1)
+        deal_gen(1)
+        quantise_wtor(1, [(0, t) for t in range(PACK)], nc.scalar.copy, "cosine00")
+        write_and_pick(0, 1)
+        quantise_wtor(1, [(1, t) for t in range(PACK)], nc.scalar.copy, "cosine01")
+        phase(0, 3)
+        write_and_pick(0, 2)
+        phase(1, 0)
+        write_and_pick(0, 3)
+        phase(1, 1)
+        turn_rows()
+        write_and_pick(1, 0)
+        phase(1, 2)
+        write_and_pick(1, 1)
+        score(0, "gained13", "cosine13")
+        phase(1, 3)
+        write_and_pick(1, 2)
+        write_and_pick(1, 3)
+        score(1, "cosine00", "cosine01")
+        for m in range(PL // P):
+            floored = ring.tile([P, PL], F32, name="floored", tag="shift")
+            nc.vector.tensor_tensor(floored[:], e[m][:], cls_sb[:], ALU.max)
+            result = keep.tile([P, PL], F32, name=f"result{m}", tag=f"cosine1{m}", align_bytes=64)
+            nc.scalar.activation(result[:], floored[:], ACT.Copy, scale=cols[:, 0, 2 * PACK + m : 2 * PACK + m + 1])
+            nc.sync.dma_start(out=out[P * m : P * (m + 1), :], in_=result[:])

@@ -24,7 +24,8 @@ PASS = P * PACK
 RUN = 8
 GROUPS = P // RUN
 QUADS = 4
-TURN_OFFSET = float(2**14)
+TWO_PI = 2.0 * math.pi
+ROUNDER = 1.5 * 2.0**23
 
 
 def tile_list_plume_quality_match_kernel(
@@ -38,22 +39,25 @@ def tile_list_plume_quality_match_kernel(
     with ExitStack() as ctx:
         keep = ctx.enter_context(tc.tile_pool(name="keep", bufs=1))
         ring = ctx.enter_context(tc.tile_pool(name="ring", bufs=2))
-        psum = ctx.enter_context(tc.psum_pool(name="psum", bufs=8))
+        psum = ctx.enter_context(tc.psum_pool(name="psum", bufs=2))
 
-        def bank(name):
-            return psum.tile([P, 512], F32, name=name, tag="bank")
+        def bank(name, tag, bufs):
+            return psum.tile([P, 512], F32, name=name, tag=tag, bufs=bufs)
 
         def wide_f32(name):
             return ring.tile([P, PACK, 512], F32, name=name, tag="wide_f32", bufs=6)
 
+        warm = keep.tile([P, 8], F32, name="warm")
+        nc.vector.memset(warm[:, 0:1], 0.0)
+        nc.scalar.activation(warm[:, 1:2], warm[:, 0:1], ACT.Sin)
         lists = {}
         for name in ("offs", "offs2", "offs3", "offs4"):
             lists[name] = keep.tile([P, S // 16], U16, name=name)
         tab_w = [keep.tile([P, T], I32, name=f"tab_w{a}") for a in range(k_passes)]
         tab_s = keep.tile([P, k_passes, T], U8, name="tab_s")
-        wph_s = keep.tile([P, k_passes, H], U8, name="wph_s")
+        wph_s = keep.tile([P, k_passes, H], U8, name="wph_s", align_bytes=64)
         wgen_s = keep.tile([P, k_passes, H], U8, name="wgen_s")
-        wph_raw = [keep.tile([P, k_passes, PASS], I32, name=f"wph_raw{b}", tag="wph_raw") for b in range(r_passes)]
+        wph_raw = [keep.tile([P, k_passes, PASS], I32, name=f"wph_raw{b}", align_bytes=64) for b in range(r_passes)]
         wgen_raw = [keep.tile([P, k_passes, PASS // 2], I32, name=f"wgen_raw{b}") for b in range(r_passes)]
         wtor_raw = {}
         for b in range(r_passes):
@@ -63,7 +67,7 @@ def tile_list_plume_quality_match_kernel(
         page = {}
         for b in range(r_passes):
             for t in range(PACK):
-                page[b, t] = keep.tile([P, T2], F32, name=f"page{b}{t}")
+                page[b, t] = keep.tile([P, T2], F32, name=f"page{b}{t}", tag=f"page{b}{t}", align_bytes=64)
         rows = keep.tile([P, r_passes * P], F32, name="rows")
         ident = keep.tile([P, P], F32, name="ident")
         cls_sb = keep.tile([P, PL], F32, name="cls_sb")
@@ -97,10 +101,10 @@ def tile_list_plume_quality_match_kernel(
             src = wtor[PASS * a : PASS * (a + 1), PASS * b : PASS * (b + 1)]
             nc.sync.dma_start(out=wtor_raw[b, a][:], in_=src.rearrange("(p j) c -> p j c", j=PACK))
 
-        def load_wgs(queue, t, quads=range(QUADS)):
+        def load_wgs(t, quads=range(QUADS)):
             src = wgs.rearrange("(g t i) c -> t g i c", t=PACK, i=RUN)[t]
             for q in quads:
-                queue.dma_start(out=wgs_sb[t][32 * q : 32 * (q + 1), :], in_=src)
+                nc.sync.dma_start(out=wgs_sb[t][32 * q : 32 * (q + 1), :], in_=src)
 
         def load_page(b, t):
             src = page0[PASS * b : PASS * (b + 1), :].rearrange("(g t i) c -> t g i c", t=PACK, i=RUN)[t]
@@ -114,15 +118,15 @@ def tile_list_plume_quality_match_kernel(
                 )
             nc.sync.dma_start(out=rows[2 * PACK : 3 * PACK, 0:P], in_=plume.rearrange("(m p) -> m p", p=P))
 
-        load_wgs(nc.gpsimd, 0, (2, 3))
-        load_wgs(nc.gpsimd, 1)
-        nc.gpsimd.memset(rows[:], 0.0)
+        rounder = keep.tile([P, 1], F32, name="rounder")
         make_identity(nc, ident[:])
+        nc.gpsimd.memset(rounder[:], ROUNDER)
+        nc.gpsimd.memset(rows[:], 0.0)
         load_list("offs", offs)
         load_list("offs2", offs2)
         load_list("offs4", offs4)
         load_list("offs3", offs3)
-        load_wgs(nc.sync, 0, (0, 1))
+        load_wgs(0, (0, 1))
         load_table(0)
         load_table(1)
         load_scales(nc.scalar, tab_s, tab_scales)
@@ -131,16 +135,18 @@ def tile_list_plume_quality_match_kernel(
         load_scales(nc.scalar, wph_s, wph_scales)
         load_wgen(0)
         load_wtor(0, 1)
-        load_scales(nc.sync, wgen_s, wgen_scales)
         load_page(0, 0)
+        load_scales(nc.scalar, wgen_s, wgen_scales)
+        load_wgs(0, (2, 3))
         load_page(0, 1)
+        load_wgs(1)
         load_wph(1)
-        load_wgen(1)
         load_wtor(1, 0)
+        load_wgen(1)
         load_wtor(1, 1)
         for t in (2, 3):
             load_page(0, t)
-            load_wgs(nc.sync, t)
+            load_wgs(t)
         load_rows()
         for t in range(PACK):
             load_page(1, t)
@@ -150,26 +156,20 @@ def tile_list_plume_quality_match_kernel(
         v_s = [keep.tile([P, S], U8, name=f"v_s{a}", align_bytes=64) for a in range(k_passes)]
         for a in range(k_passes):
             nc.vector.tensor_copy(v_s[a][:], tab_s[:, a, :].indirect(lists["offs"][:]))
-        for a in range(k_passes):
             nc.vector.tensor_copy(v_w[a][:], tab_w[a][:].bitcast(U32).indirect(lists["offs"][:]))
 
-        def deal(name, raw, words):
-            dealt = keep.tile([P, k_passes, PACK, GROUPS * words], I32, name=name, align_bytes=64)
+        def deal(name, raw, words, tag=None):
+            dealt = keep.tile([P, raw.shape[1], PACK, GROUPS * words], I32, name=name, tag=tag or name, align_bytes=64)
             nc.vector.tensor_copy(
                 out=dealt[:].rearrange("p a t (g w) -> p a t g w", w=words),
                 in_=raw.rearrange("p a (g t w) -> p a t g w", t=PACK, w=words),
             )
             return dealt
 
-        wph_sb, wgen_sb, wph_sc, wgen_sc, wtor_q, wtor_s, cosine = {}, {}, {}, {}, {}, {}, {}
+        def deal_scales(name, raw):
+            return deal(name, raw[:].rearrange("p a (b n) -> p (a b) n", b=r_passes).bitcast(I32), 2)
 
-        def deal_phase(b):
-            wph_sb[b] = deal(f"wph_d{b}", wph_raw[b][:], RUN)
-            wph_sc[b] = deal(f"wph_sd{b}", wph_s[:, :, PASS * b : PASS * (b + 1)].bitcast(I32), 2)
-
-        def deal_gen(b):
-            wgen_sb[b] = deal(f"wgen_d{b}", wgen_raw[b][:], RUN // 2)
-            wgen_sc[b] = deal(f"wgen_sd{b}", wgen_s[:, :, PASS * b : PASS * (b + 1)].bitcast(I32), 2)
+        wgen_sb, wtor_q, wtor_s, cosine = {}, {}, {}, {}
 
         def quantise_wtor(b, pieces, copy, tag=None):
             name = f"wtor{b}_{pieces[0][0]}{pieces[0][1]}"
@@ -185,52 +185,60 @@ def tile_list_plume_quality_match_kernel(
                 wtor_s[b, a, t] = scales[:, P * n : P * (n + 1)]
             nc.vector.quantize_mx(out=codes[:].bitcast(FP8X4), scales=scales[:], in_=woven[:])
 
-        def phase(b, t):
-            z = bank(f"z{b}{t}")
+        z_turned, turns, whole = {}, {}, {}
+
+        def phase_sums(b):
+            for j in range(S // P):
+                z_turned[b, j] = bank(f"z{b}{j}", f"quarter{j}", 1)
+                turns[b, j] = keep.tile([P, PACK, P], F32, name=f"turns{b}{j}", tag=f"turns{j}")
+                whole[b, j] = keep.tile([P, PACK, P], F32, name=f"whole{b}{j}", tag=f"whole{j}")
             for a in range(k_passes):
-                nc.tensor.matmul_mx(
-                    out=z[:],
-                    lhsT=wph_sb[b][:, a, t, :].bitcast(FP8X4),
-                    lhsT_scale=wph_sc[b][:, a, t, :].bitcast(U8),
-                    rhs=v_w[a][:].bitcast(FP8X4),
-                    rhs_scale=v_s[a][:],
-                    start=(a == 0),
-                    stop=(a == k_passes - 1),
-                )
-            turns = ring.tile([P, S], U32, name="turns")
-            nc.scalar.activation(turns[:], z[:], ACT.Copy, bias=TURN_OFFSET, scale=1.0 / (2.0 * math.pi))
-            shift = ring.tile([P, S], F32, name="shift", tag="shift")
-            nc.scalar.activation(shift[:], turns[:], ACT.Copy, bias=2.0 * math.pi * TURN_OFFSET, scale=-2.0 * math.pi)
-            folded = keep.tile([P, S], F32, name=f"folded{b}{t}", tag=f"work{t % 2}", align_bytes=64)
-            nc.vector.tensor_tensor(folded[:], z[:], shift[:], ALU.add)
+                for j in range(S // P):
+                    nc.tensor.matmul_mx(
+                        out=z_turned[b, j][:],
+                        lhsT=v_w[a][:, P * j : P * (j + 1)].bitcast(FP8X4),
+                        lhsT_scale=v_s[a][:, P * j : P * (j + 1)],
+                        rhs=wph_raw[b][:, a, :].bitcast(FP8X4),
+                        rhs_scale=wph_s[:, a, PASS * b : PASS * (b + 1)],
+                        start=(a == 0),
+                        stop=(a == k_passes - 1),
+                    )
+
+        def phase_turns(b, t0, t1):
+            for j in range(S // P):
+                z = z_turned[b, j][:].rearrange("p (g t i) -> p t g i", t=PACK, i=RUN)[:, t0:t1]
+                for dst, scale, bias in ((whole, -1.0 / TWO_PI, -ROUNDER), (turns, 1.0 / TWO_PI, 0.0)):
+                    nc.scalar.activation(
+                        dst[b, j][:, t0:t1, :].rearrange("p t (g i) -> p t g i", i=RUN), z, ACT.Copy, bias=bias, scale=scale
+                    )
+
+        def phase_cosine(b, t):
+            folded = bank(f"folded{b}{t}", "folded", 2)
+            for j in range(S // P):
+                terms = (whole[b, j][:, t, :], rounder[:].to_broadcast([P, P]), turns[b, j][:, t, :])
+                for n, term in enumerate(terms):
+                    nc.tensor.matmul(
+                        folded[:, P * j : P * (j + 1)], lhsT=term, rhs=ident[:],
+                        start=(n == 0), stop=(n == len(terms) - 1), is_transpose=True,
+                    )
             size = ring.tile([P, S], F32, name="size")
             nc.scalar.activation(size[:], folded[:], ACT.Abs)
             cosine[b, t] = keep.tile([P, S], F32, name=f"cosine{b}{t}", tag=f"cosine{b}{t}", align_bytes=64)
-            nc.scalar.activation(cosine[b, t][:], size[:], ACT.Sin, bias=math.pi / 2.0, scale=-1.0)
+            nc.scalar.activation(cosine[b, t][:], size[:], ACT.Sin, bias=TWO_PI / 4.0, scale=-TWO_PI)
 
         picked1, picked2 = {}, {}
 
         def write_and_pick(b, t):
-            f = bank(f"f{b}{t}")
-            for a in range(k_passes):
+            f = bank(f"f{b}{t}", "f", 2)
+            weights = [(wtor_q[b, a, t].bitcast(FP8X4), wtor_s[b, a, t], a) for a in range(k_passes)]
+            weights.extend(
+                (wgen_sb[b][:, a, t, :].bitcast(U8).bitcast(FP4X4), wgen_sc[:, r_passes * a + b, t, :].bitcast(U8), a)
+                for a in range(k_passes)
+            )
+            for n, (codes, scales, a) in enumerate(weights):
                 nc.tensor.matmul_mx(
-                    out=f[:],
-                    lhsT=wgen_sb[b][:, a, t, :].bitcast(U8).bitcast(FP4X4),
-                    lhsT_scale=wgen_sc[b][:, a, t, :].bitcast(U8),
-                    rhs=v_w[a][:].bitcast(FP8X4),
-                    rhs_scale=v_s[a][:],
-                    start=(a == 0),
-                    stop=False,
-                )
-            for a in range(k_passes):
-                nc.tensor.matmul_mx(
-                    out=f[:],
-                    lhsT=wtor_q[b, a, t].bitcast(FP8X4),
-                    lhsT_scale=wtor_s[b, a, t],
-                    rhs=v_w[a][:].bitcast(FP8X4),
-                    rhs_scale=v_s[a][:],
-                    start=False,
-                    stop=(a == k_passes - 1),
+                    out=f[:], lhsT=codes, lhsT_scale=scales, rhs=v_w[a][:].bitcast(FP8X4), rhs_scale=v_s[a][:],
+                    start=(n == 0), stop=(n == len(weights) - 1),
                 )
             last = (b, t) == (r_passes - 1, PACK - 1)
             gained = keep.tile([P, S], F32, name=f"gained{b}{t}", tag="gained13" if last else f"work{t % 2}", align_bytes=64)
@@ -242,22 +250,22 @@ def tile_list_plume_quality_match_kernel(
             nc.vector.tensor_copy(picked2[b][:, t, :], page[b, t][:].indirect(lists["offs4"][:]))
             nc.vector.tensor_copy(picked1[b][:, t, :], page[b, t][:].indirect(lists["offs3"][:]))
 
-        cols = keep.tile([P, r_passes, 16], F32, name="cols")
-        neg_bb = keep.tile([P, r_passes, PACK], F32, name="neg_bb")
         e = []
 
         def turn_rows():
-            turned = bank("turned")
+            cols = keep.tile([P, r_passes, 16], F32, name="cols", tag="page03", align_bytes=64)
+            neg_bb = keep.tile([P, r_passes, PACK], F32, name="neg_bb")
+            turned = bank("turned", "folded", 2)
             for b in range(r_passes):
                 nc.tensor.transpose(turned[:, P * b : P * (b + 1)], rows[:, P * b : P * (b + 1)], ident[:])
-            nc.scalar.copy(out=cols[:, 0, 0 : 3 * PACK], in_=turned[:, 0 : 3 * PACK])
-            nc.scalar.copy(out=cols[:, 1, 0 : 2 * PACK], in_=turned[:, P : P + 2 * PACK])
-            nc.vector.scalar_tensor_tensor(
-                out=neg_bb[:], in0=cols[:, :, 0:PACK], scalar=-1.0, in1=cols[:, :, PACK : 2 * PACK],
-                op0=ALU.mult, op1=ALU.mult,
-            )
+            halves = turned[:, 0 : r_passes * P].rearrange("p (b c) -> p b c", c=P)
+            nc.scalar.activation(cols[:, :, 0:PACK], halves[:, :, 0:PACK], ACT.Copy, scale=-1.0)
+            nc.scalar.copy(out=cols[:, :, PACK : 2 * PACK], in_=halves[:, :, PACK : 2 * PACK])
+            nc.scalar.copy(out=cols[:, 0, 2 * PACK : 3 * PACK], in_=turned[:, 2 * PACK : 3 * PACK])
+            nc.gpsimd.tensor_tensor(neg_bb[:], cols[:, :, 0:PACK], cols[:, :, PACK : 2 * PACK], ALU.mult)
             for m in range(PL // P):
-                e.append(bank(f"e{m}"))
+                e.append(bank(f"e{m}", f"quarter{m}", 1))
+            return cols, neg_bb
 
         def weave(woven, planes, count):
             nc.scalar.copy(
@@ -271,14 +279,14 @@ def tile_list_plume_quality_match_kernel(
                 bias=neg_bb[:, b, t : t + 1], scale=cols[:, b, PACK + t : PACK + t + 1],
             )
 
-        def score(b, x2_tag, x1_tag):
+        def score(b, x2_tag, x1_tag, x2_q_tag, x1_q_tag):
             early = PACK if b + 1 < r_passes else PACK - 1
             x2_planes = ring.tile([P, PACK, PL], BF16, name="x2_planes")
             x2_bf = keep.tile([P, PACK * PL], BF16, name=f"x2_bf{b}", tag=x2_tag, align_bytes=64)
             x1_bf = keep.tile([P, PACK * PL], BF16, name=f"x1_bf{b}", tag=x1_tag, align_bytes=64)
-            x1_q = keep.tile([P, PL], U32, name=f"x1_q{b}", align_bytes=64)
+            x1_q = keep.tile([P, PL], U32, name=f"x1_q{b}", tag=x1_q_tag, align_bytes=64)
             x1_s = keep.tile([P, PL], U8, name=f"x1_s{b}", align_bytes=64)
-            x2_q = keep.tile([P, PL], U32, name=f"x2_q{b}", align_bytes=64)
+            x2_q = keep.tile([P, PL], U32, name=f"x2_q{b}", tag=x2_q_tag, align_bytes=64)
             x2_s = keep.tile([P, PL], U8, name=f"x2_s{b}", align_bytes=64)
             for t in range(early):
                 centre_x2(x2_planes[:, t, :], b, t)
@@ -309,37 +317,38 @@ def tile_list_plume_quality_match_kernel(
                     stop=(b == r_passes - 1),
                 )
 
-        deal_phase(0)
-        phase(0, 0)
+        phase_sums(0)
+        phase_turns(0, 0, 1)
+        phase_cosine(0, 0)
         quantise_wtor(0, [(0, 0)], nc.vector.tensor_copy)
-        deal_gen(0)
+        wgen_sb[0] = deal("wgen_d0", wgen_raw[0][:], RUN // 2)
         quantise_wtor(0, [(1, 0)], nc.vector.tensor_copy)
-        phase(0, 1)
-        quantise_wtor(0, [(0, 1), (1, 1)], nc.scalar.copy)
+        wgen_sc = deal_scales("wgen_sc", wgen_s)
         write_and_pick(0, 0)
-        quantise_wtor(0, [(a, t) for t in (2, 3) for a in range(k_passes)], nc.scalar.copy, "cosine00")
-        phase(0, 2)
-        deal_phase(1)
-        deal_gen(1)
-        quantise_wtor(1, [(0, t) for t in range(PACK)], nc.scalar.copy, "cosine00")
+        for a in range(k_passes):
+            quantise_wtor(0, [(a, t) for t in range(1, PACK)], nc.vector.tensor_copy)
+        phase_turns(0, 1, PACK)
+        phase_cosine(0, 1)
         write_and_pick(0, 1)
-        quantise_wtor(1, [(1, t) for t in range(PACK)], nc.scalar.copy, "cosine01")
-        phase(0, 3)
+        phase_cosine(0, 2)
+        phase_cosine(0, 3)
         write_and_pick(0, 2)
-        phase(1, 0)
+        wgen_sb[1] = deal("wgen_d1", wgen_raw[1][:], RUN // 2, "page01")
+        quantise_wtor(1, [(0, t) for t in range(PACK)], nc.scalar.copy, "cosine00")
+        quantise_wtor(1, [(1, t) for t in range(PACK)], nc.scalar.copy, "cosine01")
+        phase_sums(1)
+        phase_turns(1, 0, PACK)
+        for t in range(PACK):
+            phase_cosine(1, t)
         write_and_pick(0, 3)
-        phase(1, 1)
-        turn_rows()
-        write_and_pick(1, 0)
-        phase(1, 2)
-        write_and_pick(1, 1)
-        score(0, "gained13", "cosine13")
-        phase(1, 3)
-        write_and_pick(1, 2)
+        cols, neg_bb = turn_rows()
+        for t in range(PACK - 1):
+            write_and_pick(1, t)
+        score(0, "gained13", "x1_bf0", "cosine11", "cosine12")
         write_and_pick(1, 3)
-        score(1, "cosine00", "cosine01")
+        score(1, "cosine00", "cosine01", "x2_q1", "x1_q1")
         for m in range(PL // P):
-            floored = ring.tile([P, PL], F32, name="floored", tag="shift")
+            floored = ring.tile([P, PL], F32, name="floored")
             nc.vector.tensor_tensor(floored[:], e[m][:], cls_sb[:], ALU.max)
             result = keep.tile([P, PL], F32, name=f"result{m}", tag=f"cosine1{m}", align_bytes=64)
             nc.scalar.activation(result[:], floored[:], ACT.Copy, scale=cols[:, 0, 2 * PACK + m : 2 * PACK + m + 1])

@@ -79,10 +79,10 @@ def tile_list_plume_quality_match_kernel(
         def load_list(name, src):
             nc.sync.dma_start(lists[name][:], src)
 
-        def load_scales(queue, dst, src):
+        def load_scales(dst, row0, src):
             for q in range(QUADS):
-                queue.dma_start(
-                    out=dst[32 * q : 32 * q + 4, :, :].bitcast(I32),
+                nc.scalar.dma_start(
+                    out=dst[32 * q + row0 : 32 * q + row0 + 4, :, :].bitcast(I32),
                     in_=src[:, 4 * q : 4 * q + 4, :].rearrange("a r n -> r a n").bitcast(I32),
                 )
 
@@ -101,9 +101,9 @@ def tile_list_plume_quality_match_kernel(
             src = wtor[PASS * a : PASS * (a + 1), PASS * b : PASS * (b + 1)]
             nc.sync.dma_start(out=wtor_raw[b, a][:], in_=src.rearrange("(p j) c -> p j c", j=PACK))
 
-        def load_wgs(t, quads=range(QUADS)):
+        def load_wgs(t):
             src = wgs.rearrange("(g t i) c -> t g i c", t=PACK, i=RUN)[t]
-            for q in quads:
+            for q in range(QUADS):
                 nc.sync.dma_start(out=wgs_sb[t][32 * q : 32 * (q + 1), :], in_=src)
 
         def load_page(b, t):
@@ -124,20 +124,19 @@ def tile_list_plume_quality_match_kernel(
         nc.gpsimd.memset(rows[:], 0.0)
         load_list("offs", offs)
         load_list("offs2", offs2)
-        load_list("offs4", offs4)
-        load_list("offs3", offs3)
-        load_wgs(0, (0, 1))
+        load_wgs(0)
         load_table(0)
         load_table(1)
-        load_scales(nc.scalar, tab_s, tab_scales)
+        load_scales(tab_s, 0, tab_scales)
         load_wph(0)
         load_wtor(0, 0)
-        load_scales(nc.scalar, wph_s, wph_scales)
+        load_scales(wph_s, 4, wph_scales)
         load_wgen(0)
         load_wtor(0, 1)
         load_page(0, 0)
-        load_scales(nc.scalar, wgen_s, wgen_scales)
-        load_wgs(0, (2, 3))
+        load_list("offs4", offs4)
+        load_list("offs3", offs3)
+        load_scales(wgen_s, 0, wgen_scales)
         load_page(0, 1)
         load_wgs(1)
         load_wph(1)
@@ -171,10 +170,10 @@ def tile_list_plume_quality_match_kernel(
 
         wgen_sb, wtor_q, wtor_s, cosine = {}, {}, {}, {}
 
-        def quantise_wtor(b, pieces, copy, tag=None):
+        def quantise_wtor(b, pieces, copy, tag=None, codes_tag=None):
             name = f"wtor{b}_{pieces[0][0]}{pieces[0][1]}"
             woven = keep.tile([P, len(pieces) * 512], BF16, name=name + "_bf", tag=tag or name + "_bf", align_bytes=64)
-            codes = keep.tile([P, len(pieces) * P], U32, name=name + "_q", align_bytes=64)
+            codes = keep.tile([P, len(pieces) * P], U32, name=name + "_q", tag=codes_tag or name + "_q", align_bytes=64)
             scales = keep.tile([P, len(pieces) * P], U8, name=name + "_s", align_bytes=64)
             for n, (a, t) in enumerate(pieces):
                 copy(
@@ -199,7 +198,7 @@ def tile_list_plume_quality_match_kernel(
                         lhsT=v_w[a][:, P * j : P * (j + 1)].bitcast(FP8X4),
                         lhsT_scale=v_s[a][:, P * j : P * (j + 1)],
                         rhs=wph_raw[b][:, a, :].bitcast(FP8X4),
-                        rhs_scale=wph_s[:, a, PASS * b : PASS * (b + 1)],
+                        rhs_scale=wph_s[4:P, a, PASS * b : PASS * (b + 1)],
                         start=(a == 0),
                         stop=(a == k_passes - 1),
                     )
@@ -221,6 +220,26 @@ def tile_list_plume_quality_match_kernel(
                         folded[:, P * j : P * (j + 1)], lhsT=term, rhs=ident[:],
                         start=(n == 0), stop=(n == len(terms) - 1), is_transpose=True,
                     )
+            cosine_of(folded, b, t)
+
+        def phase_direct(t):
+            z = bank(f"z0{t}", f"quarter{t}", 1)
+            for a in range(k_passes):
+                nc.tensor.matmul_mx(
+                    out=z[:], lhsT=wph_sb[:, a, t, :].bitcast(FP8X4), lhsT_scale=wph_sc[4:P, a, t, :].bitcast(U8),
+                    rhs=v_w[a][:].bitcast(FP8X4), rhs_scale=v_s[a][:], start=(a == 0), stop=(a == k_passes - 1),
+                )
+            whole_t = keep.tile([P, S], F32, name=f"whole0{t}", tag=f"whole{t}")
+            nc.scalar.activation(whole_t[:], z[:], ACT.Copy, bias=-ROUNDER, scale=-1.0 / TWO_PI)
+            turns_t = keep.tile([P, S], F32, name=f"turns0{t}", tag=f"turns{t}")
+            nc.scalar.activation(turns_t[:], z[:], ACT.Copy, scale=1.0 / TWO_PI)
+            folded = ring.tile([P, S], F32, name="folded0", tag="floored")
+            nc.vector.scalar_tensor_tensor(
+                out=folded[:], in0=whole_t[:], scalar=ROUNDER, in1=turns_t[:], op0=ALU.add, op1=ALU.add
+            )
+            cosine_of(folded, 0, t)
+
+        def cosine_of(folded, b, t):
             size = ring.tile([P, S], F32, name="size")
             nc.scalar.activation(size[:], folded[:], ACT.Abs)
             cosine[b, t] = keep.tile([P, S], F32, name=f"cosine{b}{t}", tag=f"cosine{b}{t}", align_bytes=64)
@@ -228,22 +247,31 @@ def tile_list_plume_quality_match_kernel(
 
         picked1, picked2 = {}, {}
 
-        def write_and_pick(b, t):
-            f = bank(f"f{b}{t}", "f", 2)
-            weights = [(wtor_q[b, a, t].bitcast(FP8X4), wtor_s[b, a, t], a) for a in range(k_passes)]
-            weights.extend(
+        gained = {}
+
+        def feature(b, t):
+            f = bank(f"f{b}{t}", f"quarter{t + 2}", 1) if b == 0 and t < 2 else bank(f"f{b}{t}", "f", 2)
+            torch = [(wtor_q[b, a, t].bitcast(FP8X4), wtor_s[b, a, t], a) for a in range(k_passes)]
+            generic = [
                 (wgen_sb[b][:, a, t, :].bitcast(U8).bitcast(FP4X4), wgen_sc[:, r_passes * a + b, t, :].bitcast(U8), a)
                 for a in range(k_passes)
-            )
+            ]
+            weights = torch[:-1] + generic + torch[-1:]
             for n, (codes, scales, a) in enumerate(weights):
                 nc.tensor.matmul_mx(
                     out=f[:], lhsT=codes, lhsT_scale=scales, rhs=v_w[a][:].bitcast(FP8X4), rhs_scale=v_s[a][:],
                     start=(n == 0), stop=(n == len(weights) - 1),
                 )
-            last = (b, t) == (r_passes - 1, PACK - 1)
-            gained = keep.tile([P, S], F32, name=f"gained{b}{t}", tag="gained13" if last else f"work{t % 2}", align_bytes=64)
-            nc.vector.tensor_tensor(gained[:], f[:], wgs_sb[t][:], ALU.mult)
-            nc.vector.tensor_tensor(page[b, t][:].indirect(lists["offs2"][:]), gained[:], cosine[b, t][:], ALU.mult)
+            gained[b, t] = keep.tile([P, S], F32, name=f"gained{b}{t}", tag=f"work{t % 2}", align_bytes=64)
+            if (b, t) == (0, 0):
+                nc.vector.tensor_tensor(gained[b, t][:], f[:], wgs_sb[t][:], ALU.mult)
+            else:
+                summed = ring.tile([P, S], F32, name="summed", tag="summed")
+                nc.scalar.copy(out=summed[:], in_=f[:])
+                nc.gpsimd.tensor_tensor(gained[b, t][:], summed[:], wgs_sb[t][:], ALU.mult)
+
+        def write_and_pick(b, t):
+            nc.vector.tensor_tensor(page[b, t][:].indirect(lists["offs2"][:]), gained[b, t][:], cosine[b, t][:], ALU.mult)
             if t == 0:
                 picked1[b] = wide_f32(f"picked1_{b}")
                 picked2[b] = wide_f32(f"picked2_{b}")
@@ -317,38 +345,40 @@ def tile_list_plume_quality_match_kernel(
                     stop=(b == r_passes - 1),
                 )
 
-        phase_sums(0)
-        phase_turns(0, 0, 1)
-        phase_cosine(0, 0)
+        wph_sb = deal("wph_d0", wph_raw[0][:], RUN)
+        wph_sc = deal("wph_sc", wph_s[:, :, 0:PASS].bitcast(I32), RUN // 4)
+        phase_direct(0)
         quantise_wtor(0, [(0, 0)], nc.vector.tensor_copy)
         wgen_sb[0] = deal("wgen_d0", wgen_raw[0][:], RUN // 2)
         quantise_wtor(0, [(1, 0)], nc.vector.tensor_copy)
         wgen_sc = deal_scales("wgen_sc", wgen_s)
+        feature(0, 0)
         write_and_pick(0, 0)
         for a in range(k_passes):
             quantise_wtor(0, [(a, t) for t in range(1, PACK)], nc.vector.tensor_copy)
-        phase_turns(0, 1, PACK)
-        phase_cosine(0, 1)
+        phase_direct(1)
+        feature(0, 1)
         write_and_pick(0, 1)
-        phase_cosine(0, 2)
-        phase_cosine(0, 3)
-        write_and_pick(0, 2)
-        wgen_sb[1] = deal("wgen_d1", wgen_raw[1][:], RUN // 2, "page01")
-        quantise_wtor(1, [(0, t) for t in range(PACK)], nc.scalar.copy, "cosine00")
-        quantise_wtor(1, [(1, t) for t in range(PACK)], nc.scalar.copy, "cosine01")
+        for t in (2, 3):
+            phase_direct(t)
+            feature(0, t)
+            write_and_pick(0, t)
+        wgen_sb[1] = deal("wgen_d1", wgen_raw[1][:], RUN // 2, "page00")
+        quantise_wtor(1, [(0, t) for t in range(PACK)], nc.scalar.copy, "cosine00", "page01")
+        quantise_wtor(1, [(1, t) for t in range(PACK)], nc.scalar.copy, "cosine01", "cosine02")
         phase_sums(1)
         phase_turns(1, 0, PACK)
         for t in range(PACK):
+            feature(1, t)
             phase_cosine(1, t)
-        write_and_pick(0, 3)
+            if t + 1 < PACK:
+                write_and_pick(1, t)
         cols, neg_bb = turn_rows()
-        for t in range(PACK - 1):
-            write_and_pick(1, t)
-        score(0, "gained13", "x1_bf0", "cosine11", "cosine12")
+        score(0, "x2_bf0", "x1_bf0", "cosine11", "cosine12")
         write_and_pick(1, 3)
         score(1, "cosine00", "cosine01", "x2_q1", "x1_q1")
         for m in range(PL // P):
-            floored = ring.tile([P, PL], F32, name="floored")
+            floored = ring.tile([P, PL], F32, name="floored", tag="floored")
             nc.vector.tensor_tensor(floored[:], e[m][:], cls_sb[:], ALU.max)
             result = keep.tile([P, PL], F32, name=f"result{m}", tag=f"cosine1{m}", align_bytes=64)
             nc.scalar.activation(result[:], floored[:], ACT.Copy, scale=cols[:, 0, 2 * PACK + m : 2 * PACK + m + 1])

import math
from contextlib import ExitStack

import concourse.mybir as mybir
from concourse.masks import make_identity

T, S, K, H, T2, PL = 2048, 512, 1024, 1024, 1024, 512
FLOPS = 3 * 2 * K * H * S + 2 * H * PL * PL

F32 = mybir.dt.float32
BF16 = mybir.dt.bfloat16
I32 = mybir.dt.int32
U32 = mybir.dt.uint32
U16 = mybir.dt.uint16
U8 = mybir.dt.uint8
FP8X4 = mybir.dt.float8_e4m3fn_x4
FP4X4 = mybir.dt.float4_e2m1fn_x4
ALU = mybir.AluOpType
ACT = mybir.ActivationFunctionType

P = 128
PACK = 4
PASS = P * PACK
RUN = 8
GROUPS = P // RUN
QUADS = 4
TWO_PI = 2.0 * math.pi
ROUNDER = 1.5 * 2.0**23


def tile_list_plume_quality_match_kernel(
    tc, tab_words, tab_scales, wgen_words, wgen_scales, wtor, wph_words, wph_scales,
    page0, wgs, base, bal, cls, plume, offs, offs2, offs3, offs4, out,
):
    nc = tc.nc
    k_passes = K // PASS
    r_passes = H // PASS

    with ExitStack() as ctx:
        keep = ctx.enter_context(tc.tile_pool(name="keep", bufs=1))
        ring = ctx.enter_context(tc.tile_pool(name="ring", bufs=2))
        psum = ctx.enter_context(tc.psum_pool(name="psum", bufs=2))

        def bank(name, tag, bufs):
            return psum.tile([P, 512], F32, name=name, tag=tag, bufs=bufs)

        def wide_f32(name):
            return ring.tile([P, PACK, 512], F32, name=name, tag="wide_f32", bufs=6)

        warm = keep.tile([P, 8], F32, name="warm")
        nc.vector.memset(warm[:, 0:1], 0.0)
        nc.scalar.activation(warm[:, 1:2], warm[:, 0:1], ACT.Sin)
        lists = {}
        for name in ("offs", "offs2", "offs3", "offs4"):
            lists[name] = keep.tile([P, S // 16], U16, name=name)
        tab_w = [keep.tile([P, T], I32, name=f"tab_w{a}") for a in range(k_passes)]
        tab_s = keep.tile([P, k_passes, T], U8, name="tab_s")
        wph_s = keep.tile([P, k_passes, H], U8, name="wph_s", align_bytes=64)
        wgen_s = keep.tile([P, k_passes, H], U8, name="wgen_s")
        wph_raw = [keep.tile([P, k_passes, PASS], I32, name=f"wph_raw{b}", align_bytes=64) for b in range(r_passes)]
        wgen_raw = [keep.tile([P, k_passes, PASS // 2], I32, name=f"wgen_raw{b}") for b in range(r_passes)]
        wtor_raw = {}
        for b in range(r_passes):
            for a in range(k_passes):
                wtor_raw[b, a] = wide_f32(f"wtor_raw{b}{a}")
        wgs_sb = [keep.tile([P, S], F32, name=f"wgs{t}") for t in range(PACK)]
        page = {}
        for b in range(r_passes):
            for t in range(PACK):
                page[b, t] = keep.tile([P, T2], F32, name=f"page{b}{t}", tag=f"page{b}{t}", align_bytes=64)
        rows = keep.tile([P, r_passes * P], F32, name="rows")
        ident = keep.tile([P, P], F32, name="ident")
        cls_sb = keep.tile([P, PL], F32, name="cls_sb")

        nc.vector.memset(tab_s[:].rearrange("p a n -> p (a n)").bitcast(I32), 0)
        nc.vector.memset(wph_s[:].rearrange("p a n -> p (a n)").bitcast(I32), 0)
        nc.vector.memset(wgen_s[:].rearrange("p a n -> p (a n)").bitcast(I32), 0)

        def load_list(name, src):
            nc.sync.dma_start(lists[name][:], src)

        def load_scales(dst, row0, src):
            for q in range(QUADS):
                nc.scalar.dma_start(
                    out=dst[32 * q + row0 : 32 * q + row0 + 4, :, :].bitcast(I32),
                    in_=src[:, 4 * q : 4 * q + 4, :].rearrange("a r n -> r a n").bitcast(I32),
                )

        def load_table(a):
            nc.sync.dma_start(out=tab_w[a][:], in_=tab_words[a].rearrange("p n t -> p (n t)").bitcast(I32))

        def load_wph(b):
            words = wph_words.rearrange("a p n t -> p a (n t)")[:, :, 4 * PASS * b : 4 * PASS * (b + 1)]
            nc.sync.dma_start(out=wph_raw[b][:], in_=words.bitcast(I32))

        def load_wgen(b):
            words = wgen_words.rearrange("a p n -> p a n")[:, :, 2 * PASS * b : 2 * PASS * (b + 1)]
            nc.sync.dma_start(out=wgen_raw[b][:], in_=words.bitcast(I32))

        def load_wtor(b, a):
            src = wtor[PASS * a : PASS * (a + 1), PASS * b : PASS * (b + 1)]
            nc.sync.dma_start(out=wtor_raw[b, a][:], in_=src.rearrange("(p j) c -> p j c", j=PACK))

        def load_wgs(t):
            src = wgs.rearrange("(g t i) c -> t g i c", t=PACK, i=RUN)[t]
            for q in range(QUADS):
                nc.sync.dma_start(out=wgs_sb[t][32 * q : 32 * (q + 1), :], in_=src)

        def load_page(b, t):
            src = page0[PASS * b : PASS * (b + 1), :].rearrange("(g t i) c -> t g i c", t=PACK, i=RUN)[t]
            nc.sync.dma_start(out=page[b, t][:], in_=src)

        def load_rows():
            for row0, vec in ((0, base), (PACK, bal)):
                nc.sync.dma_start(
                    out=rows[row0 : row0 + PACK, :].rearrange("t (g i) -> t g i", i=RUN),
                    in_=vec.rearrange("(g t i) -> t g i", t=PACK, i=RUN),
                )
            nc.sync.dma_start(out=rows[2 * PACK : 3 * PACK, 0:P], in_=plume.rearrange("(m p) -> m p", p=P))

        rounder = keep.tile([P, 1], F32, name="rounder")
        make_identity(nc, ident[:])
        nc.gpsimd.memset(rounder[:], ROUNDER)
        nc.gpsimd.memset(rows[:], 0.0)
        load_list("offs", offs)
        load_list("offs2", offs2)
        load_wgs(0)
        load_table(0)
        load_table(1)
        load_scales(tab_s, 0, tab_scales)
        load_wph(0)
        load_wtor(0, 0)
        load_scales(wph_s, 4, wph_scales)
        load_wgen(0)
        load_wtor(0, 1)
        load_page(0, 0)
        load_list("offs4", offs4)
        load_list("offs3", offs3)
        load_scales(wgen_s, 0, wgen_scales)
        load_page(0, 1)
        load_wgs(1)
        load_wph(1)
        load_wtor(1, 0)
        load_wgen(1)
        load_wtor(1, 1)
        for t in (2, 3):
            load_page(0, t)
            load_wgs(t)
        load_rows()
        for t in range(PACK):
            load_page(1, t)
        nc.sync.dma_start(out=cls_sb[:], in_=cls.partition_broadcast(P))

        v_w = [keep.tile([P, S], U32, name=f"v_w{a}", align_bytes=64) for a in range(k_passes)]
        v_s = [keep.tile([P, S], U8, name=f"v_s{a}", align_bytes=64) for a in range(k_passes)]
        for a in range(k_passes):
            nc.vector.tensor_copy(v_s[a][:], tab_s[:, a, :].indirect(lists["offs"][:]))
            nc.vector.tensor_copy(v_w[a][:], tab_w[a][:].bitcast(U32).indirect(lists["offs"][:]))

        def deal(name, raw, words, tag=None):
            dealt = keep.tile([P, raw.shape[1], PACK, GROUPS * words], I32, name=name, tag=tag or name, align_bytes=64)
            nc.vector.tensor_copy(
                out=dealt[:].rearrange("p a t (g w) -> p a t g w", w=words),
                in_=raw.rearrange("p a (g t w) -> p a t g w", t=PACK, w=words),
            )
            return dealt

        def deal_scales(name, raw):
            return deal(name, raw[:].rearrange("p a (b n) -> p (a b) n", b=r_passes).bitcast(I32), 2)

        wgen_sb, wtor_q, wtor_s, cosine = {}, {}, {}, {}

        def quantise_wtor(b, pieces, copy, tag=None, codes_tag=None):
            name = f"wtor{b}_{pieces[0][0]}{pieces[0][1]}"
            woven = keep.tile([P, len(pieces) * 512], BF16, name=name + "_bf", tag=tag or name + "_bf", align_bytes=64)
            codes = keep.tile([P, len(pieces) * P], U32, name=name + "_q", tag=codes_tag or name + "_q", align_bytes=64)
            scales = keep.tile([P, len(pieces) * P], U8, name=name + "_s", align_bytes=64)
            for n, (a, t) in enumerate(pieces):
                copy(
                    out=woven[:, 512 * n : 512 * (n + 1)].rearrange("p (g h i j) -> p g h j i", h=2, i=4, j=PACK),
                    in_=wtor_raw[b, a][:].rearrange("p j (g t h i) -> p t g h j i", t=PACK, h=2, i=4)[:, t],
                )
                wtor_q[b, a, t] = codes[:, P * n : P * (n + 1)]
                wtor_s[b, a, t] = scales[:, P * n : P * (n + 1)]
            nc.vector.quantize_mx(out=codes[:].bitcast(FP8X4), scales=scales[:], in_=woven[:])

        z_turned, turns, whole = {}, {}, {}

        def phase_sums(b):
            for j in range(S // P):
                z_turned[b, j] = bank(f"z{b}{j}", f"quarter{j}", 1)
                turns[b, j] = keep.tile([P, PACK, P], F32, name=f"turns{b}{j}", tag=f"turns{j}")
                whole[b, j] = keep.tile([P, PACK, P], F32, name=f"whole{b}{j}", tag=f"whole{j}")
            for a in range(k_passes):
                for j in range(S // P):
                    nc.tensor.matmul_mx(
                        out=z_turned[b, j][:],
                        lhsT=v_w[a][:, P * j : P * (j + 1)].bitcast(FP8X4),
                        lhsT_scale=v_s[a][:, P * j : P * (j + 1)],
                        rhs=wph_raw[b][:, a, :].bitcast(FP8X4),
                        rhs_scale=wph_s[4:P, a, PASS * b : PASS * (b + 1)],
                        start=(a == 0),
                        stop=(a == k_passes - 1),
                    )

        def phase_turns(b, t0, t1):
            for j in range(S // P):
                z = z_turned[b, j][:].rearrange("p (g t i) -> p t g i", t=PACK, i=RUN)[:, t0:t1]
                for dst, scale, bias in ((whole, -1.0 / TWO_PI, -ROUNDER), (turns, 1.0 / TWO_PI, 0.0)):
                    nc.scalar.activation(
                        dst[b, j][:, t0:t1, :].rearrange("p t (g i) -> p t g i", i=RUN), z, ACT.Copy, bias=bias, scale=scale
                    )

        def phase_cosine(b, t):
            folded = bank(f"folded{b}{t}", "folded", 2)
            for j in range(S // P):
                terms = (whole[b, j][:, t, :], rounder[:].to_broadcast([P, P]), turns[b, j][:, t, :])
                for n, term in enumerate(terms):
                    nc.tensor.matmul(
                        folded[:, P * j : P * (j + 1)], lhsT=term, rhs=ident[:],
                        start=(n == 0), stop=(n == len(terms) - 1), is_transpose=True,
                    )
            cosine_of(folded, b, t)

        def phase_direct(t):
            z = bank(f"z0{t}", f"quarter{t}", 1)
            for a in range(k_passes):
                nc.tensor.matmul_mx(
                    out=z[:], lhsT=wph_sb[:, a, t, :].bitcast(FP8X4), lhsT_scale=wph_sc[4:P, a, t, :].bitcast(U8),
                    rhs=v_w[a][:].bitcast(FP8X4), rhs_scale=v_s[a][:], start=(a == 0), stop=(a == k_passes - 1),
                )
            whole_t = keep.tile([P, S], F32, name=f"whole0{t}", tag=f"whole{t}")
            nc.scalar.activation(whole_t[:], z[:], ACT.Copy, bias=-ROUNDER, scale=-1.0 / TWO_PI)
            turns_t = keep.tile([P, S], F32, name=f"turns0{t}", tag=f"turns{t}")
            nc.scalar.activation(turns_t[:], z[:], ACT.Copy, scale=1.0 / TWO_PI)
            folded = ring.tile([P, S], F32, name="folded0", tag="floored")
            nc.vector.scalar_tensor_tensor(
                out=folded[:], in0=whole_t[:], scalar=ROUNDER, in1=turns_t[:], op0=ALU.add, op1=ALU.add
            )
            cosine_of(folded, 0, t)

        def cosine_of(folded, b, t):
            size = ring.tile([P, S], F32, name="size")
            nc.scalar.activation(size[:], folded[:], ACT.Abs)
            cosine[b, t] = keep.tile([P, S], F32, name=f"cosine{b}{t}", tag=f"cosine{b}{t}", align_bytes=64)
            nc.scalar.activation(cosine[b, t][:], size[:], ACT.Sin, bias=TWO_PI / 4.0, scale=-TWO_PI)

        picked1, picked2 = {}, {}

        gained = {}

        def feature(b, t):
            f = bank(f"f{b}{t}", f"quarter{t + 2}", 1) if b == 0 and t < 2 else bank(f"f{b}{t}", "f", 2)
            torch = [(wtor_q[b, a, t].bitcast(FP8X4), wtor_s[b, a, t], a) for a in range(k_passes)]
            generic = [
                (wgen_sb[b][:, a, t, :].bitcast(U8).bitcast(FP4X4), wgen_sc[:, r_passes * a + b, t, :].bitcast(U8), a)
                for a in range(k_passes)
            ]
            weights = torch[:-1] + generic + torch[-1:]
            for n, (codes, scales, a) in enumerate(weights):
                nc.tensor.matmul_mx(
                    out=f[:], lhsT=codes, lhsT_scale=scales, rhs=v_w[a][:].bitcast(FP8X4), rhs_scale=v_s[a][:],
                    start=(n == 0), stop=(n == len(weights) - 1),
                )
            gained[b, t] = keep.tile([P, S], F32, name=f"gained{b}{t}", tag=f"work{t % 2}", align_bytes=64)
            if (b, t) == (0, 0):
                nc.vector.tensor_tensor(gained[b, t][:], f[:], wgs_sb[t][:], ALU.mult)
            else:
                summed = ring.tile([P, S], F32, name="summed", tag="summed")
                nc.scalar.copy(out=summed[:], in_=f[:])
                nc.gpsimd.tensor_tensor(gained[b, t][:], summed[:], wgs_sb[t][:], ALU.mult)

        def write_and_pick(b, t):
            nc.vector.tensor_tensor(page[b, t][:].indirect(lists["offs2"][:]), gained[b, t][:], cosine[b, t][:], ALU.mult)
            if t == 0:
                picked1[b] = wide_f32(f"picked1_{b}")
                picked2[b] = wide_f32(f"picked2_{b}")
            nc.vector.tensor_copy(picked2[b][:, t, :], page[b, t][:].indirect(lists["offs4"][:]))
            nc.vector.tensor_copy(picked1[b][:, t, :], page[b, t][:].indirect(lists["offs3"][:]))

        e = []

        def turn_rows():
            cols = keep.tile([P, r_passes, 16], F32, name="cols", tag="page03", align_bytes=64)
            neg_bb = keep.tile([P, r_passes, PACK], F32, name="neg_bb")
            turned = bank("turned", "folded", 2)
            for b in range(r_passes):
                nc.tensor.transpose(turned[:, P * b : P * (b + 1)], rows[:, P * b : P * (b + 1)], ident[:])
            halves = turned[:, 0 : r_passes * P].rearrange("p (b c) -> p b c", c=P)
            nc.scalar.activation(cols[:, :, 0:PACK], halves[:, :, 0:PACK], ACT.Copy, scale=-1.0)
            nc.scalar.copy(out=cols[:, :, PACK : 2 * PACK], in_=halves[:, :, PACK : 2 * PACK])
            nc.scalar.copy(out=cols[:, 0, 2 * PACK : 3 * PACK], in_=turned[:, 2 * PACK : 3 * PACK])
            nc.gpsimd.tensor_tensor(neg_bb[:], cols[:, :, 0:PACK], cols[:, :, PACK : 2 * PACK], ALU.mult)
            for m in range(PL // P):
                e.append(bank(f"e{m}", f"quarter{m}", 1))
            return cols, neg_bb

        def weave(woven, planes, count):
            nc.scalar.copy(
                out=woven[:].rearrange("p (c i t) -> p c t i", i=4, t=PACK)[:, :, 0:count, :],
                in_=planes[:, 0:count, :].rearrange("p t (c i) -> p c t i", i=4),
            )

        def centre_x2(dst, b, t):
            nc.scalar.activation(
                dst, picked2[b][:, t, :], ACT.Identity,
                bias=neg_bb[:, b, t : t + 1], scale=cols[:, b, PACK + t : PACK + t + 1],
            )

        def score(b, x2_tag, x1_tag, x2_q_tag, x1_q_tag):
            early = PACK if b + 1 < r_passes else PACK - 1
            x2_planes = ring.tile([P, PACK, PL], BF16, name="x2_planes")
            x2_bf = keep.tile([P, PACK * PL], BF16, name=f"x2_bf{b}", tag=x2_tag, align_bytes=64)
            x1_bf = keep.tile([P, PACK * PL], BF16, name=f"x1_bf{b}", tag=x1_tag, align_bytes=64)
            x1_q = keep.tile([P, PL], U32, name=f"x1_q{b}", tag=x1_q_tag, align_bytes=64)
            x1_s = keep.tile([P, PL], U8, name=f"x1_s{b}", align_bytes=64)
            x2_q = keep.tile([P, PL], U32, name=f"x2_q{b}", tag=x2_q_tag, align_bytes=64)
            x2_s = keep.tile([P, PL], U8, name=f"x2_s{b}", align_bytes=64)
            for t in range(early):
                centre_x2(x2_planes[:, t, :], b, t)
            weave(x2_bf, x2_planes, early)
            weave(x1_bf, picked1[b], early)
            for t in range(early, PACK):
                centre_x2(x2_bf[:].rearrange("p (c t) -> p t c", t=PACK)[:, t, :], b, t)
            nc.vector.quantize_mx(out=x2_q[:].bitcast(FP8X4), scales=x2_s[:], in_=x2_bf[:])
            width = PL if early == PACK else P
            for c0 in range(0, PL, width):
                for t in range(early, PACK):
                    nc.scalar.copy(
                        out=x1_bf[:].rearrange("p (c t) -> p t c", t=PACK)[:, t, c0 : c0 + width],
                        in_=picked1[b][:, t, c0 : c0 + width],
                    )
                nc.vector.quantize_mx(
                    out=x1_q[:, c0 : c0 + width].bitcast(FP8X4), scales=x1_s[:, c0 : c0 + width],
                    in_=x1_bf[:, PACK * c0 : PACK * (c0 + width)],
                )
            for m in range(PL // P):
                nc.tensor.matmul_mx(
                    out=e[m][:],
                    lhsT=x1_q[:, P * m : P * (m + 1)].bitcast(FP8X4),
                    lhsT_scale=x1_s[:, P * m : P * (m + 1)],
                    rhs=x2_q[:].bitcast(FP8X4),
                    rhs_scale=x2_s[:],
                    start=(b == 0),
                    stop=(b == r_passes - 1),
                )

        wph_sb = deal("wph_d0", wph_raw[0][:], RUN)
        wph_sc = deal("wph_sc", wph_s[:, :, 0:PASS].bitcast(I32), RUN // 4)
        phase_direct(0)
        quantise_wtor(0, [(0, 0)], nc.vector.tensor_copy)
        wgen_sb[0] = deal("wgen_d0", wgen_raw[0][:], RUN // 2)
        quantise_wtor(0, [(1, 0)], nc.vector.tensor_copy)
        wgen_sc = deal_scales("wgen_sc", wgen_s)
        feature(0, 0)
        write_and_pick(0, 0)
        for a in range(k_passes):
            quantise_wtor(0, [(a, t) for t in range(1, PACK)], nc.vector.tensor_copy)
        phase_direct(1)
        feature(0, 1)
        write_and_pick(0, 1)
        for t in (2, 3):
            phase_direct(t)
            feature(0, t)
            write_and_pick(0, t)
        wgen_sb[1] = deal("wgen_d1", wgen_raw[1][:], RUN // 2, "page00")
        quantise_wtor(1, [(0, t) for t in range(PACK)], nc.scalar.copy, "cosine00", "page01")
        quantise_wtor(1, [(1, t) for t in range(PACK)], nc.scalar.copy, "cosine01", "cosine02")
        phase_sums(1)
        phase_turns(1, 0, PACK)
        for t in range(PACK):
            feature(1, t)
            phase_cosine(1, t)
            if t + 1 < PACK:
                write_and_pick(1, t)
        cols, neg_bb = turn_rows()
        score(0, "x2_bf0", "x1_bf0", "cosine11", "cosine12")
        write_and_pick(1, 3)
        score(1, "cosine00", "cosine01", "x2_q1", "x1_q1")
        for m in range(PL // P):
            floored = ring.tile([P, PL], F32, name="floored", tag="floored")
            nc.vector.tensor_tensor(floored[:], e[m][:], cls_sb[:], ALU.max)
            result = keep.tile([P, PL], F32, name=f"result{m}", tag=f"cosine1{m}", align_bytes=64)
            nc.scalar.activation(result[:], floored[:], ACT.Copy, scale=cols[:, 0, 2 * PACK + m : 2 * PACK + m + 1])
            nc.sync.dma_start(out=out[P * m : P * (m + 1), :], in_=result[:])
